import numpy as np
import ml_dtypes


def mxq(x, axis, fmt="e4m3"):
    dtype, down = {"e4m3": (ml_dtypes.float8_e4m3fn, 7), "e5m2": (ml_dtypes.float8_e5m2, 14)}[fmt]
    v = np.moveaxis(np.asarray(x, np.float32).astype(ml_dtypes.bfloat16).astype(np.float64), axis, -1)
    blocks = v.reshape(v.shape[:-1] + (-1, 32))
    amax = np.abs(blocks).max(-1, keepdims=True)
    byte = np.maximum(np.where(amax > 0, np.frexp(amax)[1] - 1 + 127, 0) - down, 1)
    scale = np.exp2(byte - 127.0)
    codes = (blocks / scale).astype(np.float32).astype(dtype).astype(np.float64)
    return np.moveaxis((codes * scale).reshape(v.shape), -1, axis)


WIDE = False


def mx_kscale(k):
    if not WIDE:
        return np.ones(k)
    levels = np.array([10, -10, 5, -5, 0])
    if k % 512:
        return np.exp2(np.random.permutation(np.resize(levels, k // 32))).repeat(32)
    a = np.empty((k // 512, 16))
    for p in range(k // 512):
        a[p, :8] = np.random.permutation(np.resize(levels, 8))
        for g in range(8):
            far = levels[np.abs(levels - a[p, g]) >= 10]
            a[p, g + 8] = far[np.random.randint(len(far))]
    return np.exp2(a.ravel()).repeat(32)


def f64(x):
    return np.asarray(x).astype(np.float64)


def striped(idx):
    return np.tile(idx.reshape(-1, 16).T, (8, 1)).astype(np.uint16)


def unstriped(offs):
    return offs[:16].T.reshape(-1).astype(np.int64)


def striped8(idx):
    return np.concatenate([x.reshape(-1, 16).T for x in idx]).astype(np.uint16)


def runs(offs, k):
    lists = np.stack([offs[16 * r : 16 * r + 16].T.reshape(-1) for r in range(8)]).astype(np.int64)
    return lists[np.arange(k) % 512 // 64]


def pack_weight(w):
    k, n = w.shape
    w = f64(np.asarray(w, np.float32).astype(ml_dtypes.bfloat16)).reshape(k // 32, 32, n)
    amax = np.abs(w).max(1)
    byte = np.clip(np.where(amax > 0, np.frexp(amax)[1] - 1 + 127 - 7, 1), 1, 254)
    scaled = (w * np.exp2(127.0 - byte)[:, None, :]).reshape(k, n).astype(np.float32)
    words = np.ascontiguousarray(scaled.reshape(k // 512, 128, 4, n).transpose(0, 1, 3, 2)).astype(ml_dtypes.float8_e4m3fn).view(np.uint8)
    return words, np.ascontiguousarray(byte.astype(np.uint8).reshape(k // 512, 16, n))


def unpack_weight(words, scales):
    g, p, n, _ = words.shape
    vals = np.ascontiguousarray(words).view(ml_dtypes.float8_e4m3fn).astype(np.float64) * np.repeat(np.exp2(scales.astype(np.float64) - 127.0), 8, axis=1)[..., None]
    return vals.transpose(0, 1, 3, 2).reshape(g * 512, n)

def planes(y):
    n, m = y.shape
    v = y.astype(np.float32).astype(ml_dtypes.bfloat16).astype(np.float64).reshape(n // 32, 32, m)
    top = np.abs(v).max(1)
    byte = np.clip(np.where(top > 0, np.frexp(top)[1] - 1 + 127 - 7, 1), 1, 254)
    codes = (v * np.exp2(127.0 - byte)[:, None, :]).reshape(n, m).astype(np.float32).astype(ml_dtypes.float8_e4m3fn).view(np.uint8)
    words = codes.reshape(n // 512, 128, 4, m).transpose(0, 1, 3, 2)
    return np.ascontiguousarray(words), np.ascontiguousarray(byte.astype(np.uint8).reshape(n // 512, 16, m))


K, T, S, N, G, H = 512, 2048, 512, 512, 2048, 512


def setup_inputs():
    n = np.random.standard_normal
    s = mx_kscale(K)[:, None]
    u = mx_kscale(H)
    packed_xT = pack_weight(n((K, T)) * s)
    packed_dT = pack_weight(n((K, G)) / s)
    packed_w1 = pack_weight(n((H, N)) / np.sqrt(H) / u[:, None])
    return {
        "x_words": packed_xT[0],
        "x_scales": packed_xT[1],
        "d_words": packed_dT[0],
        "d_scales": packed_dT[1],
        "gn": (np.random.uniform(0.5, 1.5, (H, 1)) * u[:, None]).astype(np.float32),
        "w1_words": packed_w1[0],
        "w1_scales": packed_w1[1],
        "offs": striped(np.random.permutation(T)[:S]),
        "kidx": striped8(np.random.randint(0, G, (8, H))),
        "n1": striped8(np.stack([np.random.permutation(S) for _ in range(8)])),
        "n2": striped8(np.stack([np.random.permutation(S) for _ in range(8)])),
    }


def reference(x_words, x_scales, d_words, d_scales, gn, w1_words, w1_scales, offs, kidx, n1, n2):
    d_kidx = unpack_weight(d_words, d_scales)[np.arange(K)[:, None], runs(kidx, K)]
    xq = unpack_weight(x_words, x_scales)[:, unstriped(offs)]
    s = 0.0625 * (d_kidx.T @ xq)
    ex = np.exp(0.5 * s)
    z = f64(gn) * ((2.0 * ex) / (ex + ex[np.arange(H)[:, None], runs(n1, H)] + ex[np.arange(H)[:, None], runs(n2, H)]))
    out_0 = unpack_weight(w1_words, w1_scales).T @ mxq(z, 0, "e4m3")
    return (out_0,) + planes(out_0)

@@ -1,0 +1,218 @@
+from contextlib import ExitStack
+
+import concourse.mybir as mybir
+
+K, T, S, N, G, H = 512, 2048, 512, 512, 2048, 512
+FLOPS = 2 * K * H * S + 2 * H * N * S
+
+F32 = mybir.dt.float32
+BF16 = mybir.dt.bfloat16
+I32 = mybir.dt.int32
+U32 = mybir.dt.uint32
+U16 = mybir.dt.uint16
+U8 = mybir.dt.uint8
+FP8X4 = mybir.dt.float8_e4m3fn_x4
+ACT = mybir.ActivationFunctionType
+ALU = mybir.AluOpType
+
+P = 128
+PACK = 4
+UNIT = 128
+CHUNKS = ((0, 256), (256, 384), (384, 512))
+
+
+def tile_picked_localsm_none_po_kernel(tc, x_words, x_scales, d_words, d_scales, gn, w1_words, w1_scales, offs, kidx, n1, n2, out_0, out_1, out_2):
+    nc = tc.nc
+    with ExitStack() as ctx:
+        lists = ctx.enter_context(tc.tile_pool(name="lists", bufs=1))
+        held = ctx.enter_context(tc.tile_pool(name="held", bufs=1))
+        psum = ctx.enter_context(tc.psum_pool(name="psum", bufs=1))
+
+        def sb(name, shape, dtype, tag=None):
+            return held.tile(shape, dtype, name=name, tag=tag or name, align_bytes=64)
+
+        def words_of(ap):
+            return ap[0].rearrange("p n t -> p (n t)").bitcast(I32)
+
+        kidx_t = lists.tile([P, H // 16], U16, name="kidx_t")
+        offs_t = lists.tile([P, S // 16], U16, name="offs_t")
+        n1_t = lists.tile([P, S // 16], U16, name="n1_t")
+        n2_t = lists.tile([P, S // 16], U16, name="n2_t")
+
+        d_sw = sb("d_sw", [P, G], U8)
+        x_sw = sb("x_sw", [P, T], U8)
+        d_ww = sb("d_ww", [P, G], I32)
+        x_ww = sb("x_ww", [P, T], I32)
+        planes = sb("planes", [P, H + S], U8)
+        gn_t = sb("gn_t", [P, PACK], F32)
+
+        nc.vector.memset(d_sw[:].bitcast(I32), 0)
+        nc.gpsimd.memset(x_sw[:].bitcast(I32), 0)
+        nc.vector.memset(planes[:].bitcast(I32), 0)
+
+        nc.sync.dma_start(kidx_t[:], kidx)
+        nc.sync.dma_start(offs_t[:], offs)
+        nc.sync.dma_start(n1_t[:], n1)
+        nc.sync.dma_start(n2_t[:], n2)
+        nc.sync.dma_start(gn_t[:], gn.rearrange("(p t) o -> p (t o)", t=PACK))
+        nc.sync.dma_start(d_sw[0:P:8, :].bitcast(I32), d_scales[0].bitcast(I32))
+        nc.sync.dma_start(x_sw[0:P:8, :].bitcast(I32), x_scales[0].bitcast(I32))
+        nc.sync.dma_start(d_ww[:], words_of(d_words))
+        nc.sync.dma_start(x_ww[:], words_of(x_words))
+
+        d_sg = sb("d_sg", [P, H], U8)
+        x_sg = sb("x_sg", [P, S], U8)
+        staged = sb("staged", [P, H + S], U8)
+        nc.vector.tensor_copy(d_sg[:], d_sw[:].indirect(kidx_t[:]))
+        nc.vector.tensor_copy(x_sg[:], x_sw[:].indirect(offs_t[:]))
+        nc.vector.tensor_copy(
+            staged[:, 0:H].rearrange("p (t m) -> p t m", t=PACK), d_sg[:].rearrange("p (m t) -> p t m", t=PACK)
+        )
+        nc.vector.tensor_copy(staged[:, H : H + S].bitcast(I32), x_sg[:].bitcast(I32))
+        for q in range(4):
+            nc.scalar.dma_start(
+                planes[32 * q : 32 * q + 4, :].bitcast(I32), staged[32 * q : 32 * q + 32 : 8, :].bitcast(I32)
+            )
+
+        w_sw = sb("w_sw", [P, N], U8, tag="x_sg")
+        nc.gpsimd.memset(w_sw[:].bitcast(I32), 0)
+        for q in range(4):
+            nc.sync.dma_start(w_sw[32 * q : 32 * q + 4, :].bitcast(I32), w1_scales[0, 4 * q : 4 * q + 4, :].bitcast(I32))
+
+        d_wg = sb("d_wg", [P, H], I32)
+        x_wg = sb("x_wg", [P, S], I32)
+        d_wq = sb("d_wq", [P, H], I32)
+        nc.vector.tensor_copy(d_wg[:].bitcast(U32), d_ww[:].bitcast(U32).indirect(kidx_t[:]))
+        nc.vector.tensor_copy(
+            d_wq[:].rearrange("p (t m) -> p t m", t=PACK), d_wg[:].rearrange("p (m t) -> p t m", t=PACK)
+        )
+        w_ww = sb("w_ww", [P, N], I32, tag="d_ww")
+        nc.sync.dma_start(w_ww[:], words_of(w1_words))
+        half = S // 2
+        for lo in (0, half):
+            nc.vector.tensor_copy(
+                x_wg[:, lo : lo + half].bitcast(U32),
+                x_ww[:].bitcast(U32).indirect(offs_t[:, lo // 16 : (lo + half) // 16]),
+            )
+
+        w_wq = sb("w_wq", [P, N], I32)
+        w_sq = sb("w_sq", [P, N], U8)
+
+        ex = [sb(f"ex{t}", [P, S], F32) for t in range(PACK)]
+        own = [[sb(f"own{c}_{t}", [P, hi - lo], F32) for t in range(PACK)] for c, (lo, hi) in enumerate(CHUNKS[:1])]
+        rest = [sb(f"rest{t}", [P, S - CHUNKS[0][1]], F32) for t in range(PACK)]
+        first = CHUNKS[0][1]
+        for t in range(PACK):
+            cols = slice(P * t, P * (t + 1))
+            pieces = ((0, half), (half, S)) if t == 0 else ((0, S),)
+            for lo, hi in pieces:
+                s_ps = psum.tile([P, hi - lo], F32, name=f"s{t}_{lo}", tag=f"bank{t}" if lo == 0 else "bank4")
+                nc.tensor.matmul_mx(
+                    s_ps[:],
+                    lhsT=d_wq[:, cols].bitcast(FP8X4),
+                    lhsT_scale=planes[:, cols],
+                    rhs=x_wg[:, lo:hi].bitcast(FP8X4),
+                    rhs_scale=planes[:, H + lo : H + hi],
+                    start=True,
+                    stop=True,
+                )
+                nc.scalar.activation(ex[t][:, lo:hi], s_ps[:], ACT.Exp, scale=1.0 / 32.0)
+                if lo == 0:
+                    nc.scalar.activation(own[0][t][:], s_ps[:, 0:first], ACT.Exp, scale=1.0 / 32.0)
+            nc.sync.dma_start(rest[t][:], ex[t][:, first:S])
+
+        nc.vector.tensor_copy(
+            w_wq[:].rearrange("p (t m) -> p t m", t=PACK), w_ww[:].rearrange("p (m t) -> p t m", t=PACK)
+        )
+        nc.vector.tensor_copy(
+            w_sq[:].rearrange("p (t m) -> p t m", t=PACK), w_sw[:].rearrange("p (m t) -> p t m", t=PACK)
+        )
+
+        den, r2, zq, zs = {}, {}, {}, {}
+        o_codes = sb("o_codes", [P, S], I32)
+        o_scales = sb("o_scales", [P, S], U8)
+        out_rows = out_0.rearrange("(p t) j -> p t j", t=PACK)
+
+        def gathers(c):
+            lo, hi = CHUNKS[c]
+            den[c] = sb(f"den{c}", [P, PACK, hi - lo], F32)
+            part = sb(f"part{c}", [P, PACK, hi - lo], F32)
+            cols = slice(lo // 16, hi // 16)
+            for t in range(PACK):
+                mine = own[0][t][:] if c == 0 else rest[t][:, lo - first : hi - first]
+                nc.vector.tensor_tensor(part[:, t, :], ex[t][:].indirect(n1_t[:, cols]), mine, ALU.add)
+                if t > 0:
+                    nc.vector.tensor_tensor(den[c][:, t - 1, :], ex[t - 1][:].indirect(n2_t[:, cols]), part[:, t - 1, :], ALU.add)
+            t = PACK - 1
+            nc.vector.tensor_tensor(den[c][:, t, :], ex[t][:].indirect(n2_t[:, cols]), part[:, t, :], ALU.add)
+
+        exg_all = sb("exg_all", [P, PACK, S], F32)
+
+        def weigh():
+            for t in range(PACK):
+                nc.scalar.activation(exg_all[:, t, :], ex[t][:], ACT.Copy, scale=gn_t[:, t : t + 1])
+
+        def invert(c):
+            lo, hi = CHUNKS[c]
+            r = sb(f"r{c}", [P, PACK, hi - lo], F32)
+            r2[c] = sb(f"r2{c}", [P, PACK, hi - lo], F32)
+            nc.scalar.activation(r[:], den[c][:], ACT.Abs_reciprocal_sqrt, scale=0.5)
+            nc.scalar.activation(r2[c][:], r[:], ACT.Square)
+
+        def share(c):
+            lo, hi = CHUNKS[c]
+            w = hi - lo
+            zb = sb(f"zb{c}", [P, w * PACK], BF16)
+            zq[c] = sb(f"zq{c}", [P, w], I32)
+            zs[c] = sb(f"zs{c}", [P, w], U8)
+            nc.vector.tensor_tensor(
+                zb[:].rearrange("p (c i t) -> p c t i", i=4, t=PACK),
+                r2[c][:].rearrange("p t (c i) -> p c t i", i=4),
+                exg_all[:, :, lo:hi].rearrange("p t (c i) -> p c t i", i=4),
+                ALU.mult,
+            )
+            nc.vector.quantize_mx(out=zq[c][:].bitcast(FP8X4), scales=zs[c][:], in_=zb[:])
+
+        def finish(c, round_on_scalar):
+            lo, hi = CHUNKS[c]
+            for j0 in range(lo, hi, UNIT):
+                u = j0 // UNIT
+                o_ps = psum.tile([P, PACK, UNIT], F32, name=f"o{u}", tag=f"bank{(u + 5) % 8}")
+                mine = slice(j0 - lo, j0 - lo + UNIT)
+                for t in range(PACK):
+                    cols = slice(P * t, P * (t + 1))
+                    nc.tensor.matmul_mx(
+                        o_ps[:, t, :],
+                        lhsT=w_wq[:, cols].bitcast(FP8X4),
+                        lhsT_scale=w_sq[:, cols],
+                        rhs=zq[c][:, mine].bitcast(FP8X4),
+                        rhs_scale=zs[c][:, mine],
+                        start=True,
+                        stop=True,
+                    )
+                o_sb = sb(f"o_sb{u}", [P, PACK, UNIT], F32)
+                ob = sb(f"ob{u}", [P, UNIT * PACK], BF16)
+                ob_view = ob[:].rearrange("p (c i t) -> p c t i", i=4, t=PACK)
+                nc.scalar.copy(o_sb[:], o_ps[:])
+                nc.sync.dma_start(out_rows[:, :, j0 : j0 + UNIT], o_sb[:])
+                if round_on_scalar:
+                    nc.scalar.copy(ob_view, o_ps[:].rearrange("p t (c i) -> p c t i", i=4))
+                else:
+                    nc.vector.tensor_copy(ob_view, o_sb[:].rearrange("p t (c i) -> p c t i", i=4))
+                nc.vector.quantize_mx(
+                    out=o_codes[:, j0 : j0 + UNIT].bitcast(FP8X4), scales=o_scales[:, j0 : j0 + UNIT], in_=ob[:]
+                )
+            nc.sync.dma_start(words_of(out_1)[:, lo:hi], o_codes[:, lo:hi])
+
+        weigh()
+        for c in range(len(CHUNKS)):
+            gathers(c)
+        for c in range(len(CHUNKS)):
+            invert(c)
+        for c in range(len(CHUNKS)):
+            share(c)
+        for c in range(len(CHUNKS)):
+            finish(c, False)
+        for q in range(4):
+            eng = nc.sync if q % 2 == 0 else nc.scalar
+            eng.dma_start(out_2[0, 4 * q : 4 * q + 4, :].bitcast(I32), o_scales[32 * q : 32 * q + 4, :].bitcast(I32))

@@ -46,8 +46,8 @@ def tile_picked_localsm_none_po_kernel(tc, x_words, x_scales, d_words, d_scales,
         planes = sb("planes", [P, H + S], U8)
         gn_t = sb("gn_t", [P, PACK], F32)
 
-        nc.vector.memset(d_sw[:].bitcast(I32), 0)
-        nc.gpsimd.memset(x_sw[:].bitcast(I32), 0)
+        nc.gpsimd.memset(d_sw[:].bitcast(I32), 0)
+        nc.vector.memset(x_sw[:].bitcast(I32), 0)
         nc.vector.memset(planes[:].bitcast(I32), 0)
 
         nc.sync.dma_start(kidx_t[:], kidx)
@@ -66,7 +66,8 @@ def tile_picked_localsm_none_po_kernel(tc, x_words, x_scales, d_words, d_scales,
         nc.vector.tensor_copy(d_sg[:], d_sw[:].indirect(kidx_t[:]))
         nc.vector.tensor_copy(x_sg[:], x_sw[:].indirect(offs_t[:]))
         nc.vector.tensor_copy(
-            staged[:, 0:H].rearrange("p (t m) -> p t m", t=PACK), d_sg[:].rearrange("p (m t) -> p t m", t=PACK)
+            staged[:, 0:H].rearrange("p (t c i) -> p c t i", t=PACK, i=16),
+            d_sg[:].rearrange("p (c i t) -> p c t i", t=PACK, i=16),
         )
         nc.vector.tensor_copy(staged[:, H : H + S].bitcast(I32), x_sg[:].bitcast(I32))
         for q in range(4):
@@ -84,7 +85,8 @@ def tile_picked_localsm_none_po_kernel(tc, x_words, x_scales, d_words, d_scales,
         d_wq = sb("d_wq", [P, H], I32)
         nc.vector.tensor_copy(d_wg[:].bitcast(U32), d_ww[:].bitcast(U32).indirect(kidx_t[:]))
         nc.vector.tensor_copy(
-            d_wq[:].rearrange("p (t m) -> p t m", t=PACK), d_wg[:].rearrange("p (m t) -> p t m", t=PACK)
+            d_wq[:].rearrange("p (t c i) -> p c t i", t=PACK, i=4),
+            d_wg[:].rearrange("p (c i t) -> p c t i", t=PACK, i=4),
         )
         w_ww = sb("w_ww", [P, N], I32, tag="d_ww")
         nc.sync.dma_start(w_ww[:], words_of(w1_words))
@@ -122,10 +124,12 @@ def tile_picked_localsm_none_po_kernel(tc, x_words, x_scales, d_words, d_scales,
             nc.sync.dma_start(rest[t][:], ex[t][:, first:S])
 
         nc.vector.tensor_copy(
-            w_wq[:].rearrange("p (t m) -> p t m", t=PACK), w_ww[:].rearrange("p (m t) -> p t m", t=PACK)
+            w_wq[:].rearrange("p (t c i) -> p c t i", t=PACK, i=4),
+            w_ww[:].rearrange("p (c i t) -> p c t i", t=PACK, i=4),
         )
         nc.vector.tensor_copy(
-            w_sq[:].rearrange("p (t m) -> p t m", t=PACK), w_sw[:].rearrange("p (m t) -> p t m", t=PACK)
+            w_sq[:].rearrange("p (t c i) -> p c t i", t=PACK, i=16),
+            w_sw[:].rearrange("p (c i t) -> p c t i", t=PACK, i=16),
         )
 
         den, r2, zq, zs = {}, {}, {}, {}
@@ -159,60 +163,74 @@ def tile_picked_localsm_none_po_kernel(tc, x_words, x_scales, d_words, d_scales,
             nc.scalar.activation(r[:], den[c][:], ACT.Abs_reciprocal_sqrt, scale=0.5)
             nc.scalar.activation(r2[c][:], r[:], ACT.Square)
 
-        def share(c):
-            lo, hi = CHUNKS[c]
-            w = hi - lo
-            zb = sb(f"zb{c}", [P, w * PACK], BF16)
-            zq[c] = sb(f"zq{c}", [P, w], I32)
-            zs[c] = sb(f"zs{c}", [P, w], U8)
+        units = S // UNIT
+        zb = {}
+
+        def share(u):
+            c = [lo <= u * UNIT < hi for lo, hi in CHUNKS].index(True)
+            j0 = u * UNIT - CHUNKS[c][0]
+            zb[u] = sb(f"zb{u}", [P, UNIT * PACK], BF16)
             nc.vector.tensor_tensor(
-                zb[:].rearrange("p (c i t) -> p c t i", i=4, t=PACK),
-                r2[c][:].rearrange("p t (c i) -> p c t i", i=4),
-                exg_all[:, :, lo:hi].rearrange("p t (c i) -> p c t i", i=4),
+                zb[u][:].rearrange("p (c i t) -> p c t i", i=2, t=PACK),
+                r2[c][:, :, j0 : j0 + UNIT].rearrange("p t (c i) -> p c t i", i=2),
+                exg_all[:, :, u * UNIT : (u + 1) * UNIT].rearrange("p t (c i) -> p c t i", i=2),
                 ALU.mult,
             )
-            nc.vector.quantize_mx(out=zq[c][:].bitcast(FP8X4), scales=zs[c][:], in_=zb[:])
 
-        def finish(c, round_on_scalar):
-            lo, hi = CHUNKS[c]
-            for j0 in range(lo, hi, UNIT):
-                u = j0 // UNIT
-                o_ps = psum.tile([P, PACK, UNIT], F32, name=f"o{u}", tag=f"bank{(u + 5) % 8}")
-                mine = slice(j0 - lo, j0 - lo + UNIT)
-                for t in range(PACK):
-                    cols = slice(P * t, P * (t + 1))
-                    nc.tensor.matmul_mx(
-                        o_ps[:, t, :],
-                        lhsT=w_wq[:, cols].bitcast(FP8X4),
-                        lhsT_scale=w_sq[:, cols],
-                        rhs=zq[c][:, mine].bitcast(FP8X4),
-                        rhs_scale=zs[c][:, mine],
-                        start=True,
-                        stop=True,
-                    )
-                o_sb = sb(f"o_sb{u}", [P, PACK, UNIT], F32)
-                ob = sb(f"ob{u}", [P, UNIT * PACK], BF16)
-                ob_view = ob[:].rearrange("p (c i t) -> p c t i", i=4, t=PACK)
-                nc.scalar.copy(o_sb[:], o_ps[:])
-                nc.sync.dma_start(out_rows[:, :, j0 : j0 + UNIT], o_sb[:])
-                if round_on_scalar:
-                    nc.scalar.copy(ob_view, o_ps[:].rearrange("p t (c i) -> p c t i", i=4))
-                else:
-                    nc.vector.tensor_copy(ob_view, o_sb[:].rearrange("p t (c i) -> p c t i", i=4))
-                nc.vector.quantize_mx(
-                    out=o_codes[:, j0 : j0 + UNIT].bitcast(FP8X4), scales=o_scales[:, j0 : j0 + UNIT], in_=ob[:]
+        def pack(u):
+            zq[u] = sb(f"zq{u}", [P, UNIT], I32)
+            zs[u] = sb(f"zs{u}", [P, UNIT], U8)
+            nc.vector.quantize_mx(out=zq[u][:].bitcast(FP8X4), scales=zs[u][:], in_=zb[u][:])
+
+        o_sb, ob = {}, {}
+
+        def product(u):
+            o_ps = psum.tile([P, PACK, UNIT], F32, name=f"o{u}", tag=f"bank{(u + 5) % 8}")
+            for t in range(PACK):
+                cols = slice(P * t, P * (t + 1))
+                nc.tensor.matmul_mx(
+                    o_ps[:, t, :],
+                    lhsT=w_wq[:, cols].bitcast(FP8X4),
+                    lhsT_scale=w_sq[:, cols],
+                    rhs=zq[u][:].bitcast(FP8X4),
+                    rhs_scale=zs[u][:],
+                    start=True,
+                    stop=True,
                 )
-            nc.sync.dma_start(words_of(out_1)[:, lo:hi], o_codes[:, lo:hi])
+            o_sb[u] = sb(f"o_sb{u}", [P, PACK, UNIT], F32)
+            nc.scalar.copy(o_sb[u][:], o_ps[:])
+            nc.sync.dma_start(out_rows[:, :, u * UNIT : (u + 1) * UNIT], o_sb[u][:])
+
+        def round_out(u):
+            ob[u] = sb(f"ob{u}", [P, UNIT * PACK], BF16)
+            nc.vector.tensor_copy(
+                ob[u][:].rearrange("p (c i t) -> p c t i", i=2, t=PACK),
+                o_sb[u][:].rearrange("p t (c i) -> p c t i", i=2),
+            )
+
+        def pack_out(u):
+            cols = slice(u * UNIT, (u + 1) * UNIT)
+            nc.vector.quantize_mx(out=o_codes[:, cols].bitcast(FP8X4), scales=o_scales[:, cols], in_=ob[u][:])
+            if u % 2 == 1:
+                pair = slice((u - 1) * UNIT, (u + 1) * UNIT)
+                nc.sync.dma_start(words_of(out_1)[:, pair], o_codes[:, pair])
 
         weigh()
         for c in range(len(CHUNKS)):
             gathers(c)
         for c in range(len(CHUNKS)):
             invert(c)
-        for c in range(len(CHUNKS)):
-            share(c)
-        for c in range(len(CHUNKS)):
-            finish(c, False)
+        for u in range(units + 1):
+            if u < units:
+                share(u)
+            if u > 0:
+                pack(u - 1)
+                product(u - 1)
+        for u in range(units + 1):
+            if u < units:
+                round_out(u)
+            if u > 0:
+                pack_out(u - 1)
         for q in range(4):
             eng = nc.sync if q % 2 == 0 else nc.scalar
             eng.dma_start(out_2[0, 4 * q : 4 * q + 4, :].bitcast(I32), o_scales[32 * q : 32 * q + 4, :].bitcast(I32))

@@ -18,7 +18,7 @@ ALU = mybir.AluOpType
 P = 128
 PACK = 4
 UNIT = 128
-CHUNKS = ((0, 256), (256, 384), (384, 512))
+CHUNKS = ((0, 256), (256, 512))
 
 
 def tile_picked_localsm_none_po_kernel(tc, x_words, x_scales, d_words, d_scales, gn, w1_words, w1_scales, offs, kidx, n1, n2, out_0, out_1, out_2):
@@ -43,42 +43,44 @@ def tile_picked_localsm_none_po_kernel(tc, x_words, x_scales, d_words, d_scales,
         x_sw = sb("x_sw", [P, T], U8)
         d_ww = sb("d_ww", [P, G], I32)
         x_ww = sb("x_ww", [P, T], I32)
-        planes = sb("planes", [P, H + S], U8)
+        planes = sb("planes", [P, H], U8)
+        w_sw = sb("w_sw", [P, N], U8)
+        w_ww = sb("w_ww", [P, N], I32)
         gn_t = sb("gn_t", [P, PACK], F32)
 
         nc.gpsimd.memset(d_sw[:].bitcast(I32), 0)
         nc.vector.memset(x_sw[:].bitcast(I32), 0)
         nc.vector.memset(planes[:].bitcast(I32), 0)
+        nc.vector.memset(w_sw[:].bitcast(I32), 0)
 
         nc.sync.dma_start(kidx_t[:], kidx)
         nc.sync.dma_start(offs_t[:], offs)
-        nc.sync.dma_start(n1_t[:], n1)
-        nc.sync.dma_start(n2_t[:], n2)
-        nc.sync.dma_start(gn_t[:], gn.rearrange("(p t) o -> p (t o)", t=PACK))
         nc.sync.dma_start(d_sw[0:P:8, :].bitcast(I32), d_scales[0].bitcast(I32))
-        nc.sync.dma_start(x_sw[0:P:8, :].bitcast(I32), x_scales[0].bitcast(I32))
+        for q in range(4):
+            nc.sync.dma_start(x_sw[32 * q : 32 * q + 4, :].bitcast(I32), x_scales[0, 4 * q : 4 * q + 4, :].bitcast(I32))
         nc.sync.dma_start(d_ww[:], words_of(d_words))
         nc.sync.dma_start(x_ww[:], words_of(x_words))
+        nc.sync.dma_start(n1_t[:], n1)
+        nc.sync.dma_start(n2_t[:], n2)
 
         d_sg = sb("d_sg", [P, H], U8)
         x_sg = sb("x_sg", [P, S], U8)
-        staged = sb("staged", [P, H + S], U8)
+        staged = sb("staged", [P, H], U8)
         nc.vector.tensor_copy(d_sg[:], d_sw[:].indirect(kidx_t[:]))
-        nc.vector.tensor_copy(x_sg[:], x_sw[:].indirect(offs_t[:]))
         nc.vector.tensor_copy(
-            staged[:, 0:H].rearrange("p (t c i) -> p c t i", t=PACK, i=16),
+            staged[:].rearrange("p (t c i) -> p c t i", t=PACK, i=16),
             d_sg[:].rearrange("p (c i t) -> p c t i", t=PACK, i=16),
         )
-        nc.vector.tensor_copy(staged[:, H : H + S].bitcast(I32), x_sg[:].bitcast(I32))
         for q in range(4):
             nc.scalar.dma_start(
                 planes[32 * q : 32 * q + 4, :].bitcast(I32), staged[32 * q : 32 * q + 32 : 8, :].bitcast(I32)
             )
+        nc.vector.tensor_copy(x_sg[:], x_sw[:].indirect(offs_t[:]))
 
-        w_sw = sb("w_sw", [P, N], U8, tag="x_sg")
-        nc.gpsimd.memset(w_sw[:].bitcast(I32), 0)
+        nc.sync.dma_start(w_ww[:], words_of(w1_words))
         for q in range(4):
             nc.sync.dma_start(w_sw[32 * q : 32 * q + 4, :].bitcast(I32), w1_scales[0, 4 * q : 4 * q + 4, :].bitcast(I32))
+        nc.sync.dma_start(gn_t[:], gn.rearrange("(p t) o -> p (t o)", t=PACK))
 
         d_wg = sb("d_wg", [P, H], I32)
         x_wg = sb("x_wg", [P, S], I32)
@@ -88,8 +90,6 @@ def tile_picked_localsm_none_po_kernel(tc, x_words, x_scales, d_words, d_scales,
             d_wq[:].rearrange("p (t c i) -> p c t i", t=PACK, i=4),
             d_wg[:].rearrange("p (c i t) -> p c t i", t=PACK, i=4),
         )
-        w_ww = sb("w_ww", [P, N], I32, tag="d_ww")
-        nc.sync.dma_start(w_ww[:], words_of(w1_words))
         half = S // 2
         for lo in (0, half):
             nc.vector.tensor_copy(
@@ -101,9 +101,7 @@ def tile_picked_localsm_none_po_kernel(tc, x_words, x_scales, d_words, d_scales,
         w_sq = sb("w_sq", [P, N], U8)
 
         ex = [sb(f"ex{t}", [P, S], F32) for t in range(PACK)]
-        own = [[sb(f"own{c}_{t}", [P, hi - lo], F32) for t in range(PACK)] for c, (lo, hi) in enumerate(CHUNKS[:1])]
-        rest = [sb(f"rest{t}", [P, S - CHUNKS[0][1]], F32) for t in range(PACK)]
-        first = CHUNKS[0][1]
+        own = [sb(f"own{t}", [P, S], F32) for t in range(PACK)]
         for t in range(PACK):
             cols = slice(P * t, P * (t + 1))
             pieces = ((0, half), (half, S)) if t == 0 else ((0, S),)
@@ -114,14 +112,15 @@ def tile_picked_localsm_none_po_kernel(tc, x_words, x_scales, d_words, d_scales,
                     lhsT=d_wq[:, cols].bitcast(FP8X4),
                     lhsT_scale=planes[:, cols],
                     rhs=x_wg[:, lo:hi].bitcast(FP8X4),
-                    rhs_scale=planes[:, H + lo : H + hi],
+                    rhs_scale=x_sg[:, lo:hi],
                     start=True,
                     stop=True,
                 )
                 nc.scalar.activation(ex[t][:, lo:hi], s_ps[:], ACT.Exp, scale=1.0 / 32.0)
-                if lo == 0:
-                    nc.scalar.activation(own[0][t][:], s_ps[:, 0:first], ACT.Exp, scale=1.0 / 32.0)
-            nc.sync.dma_start(rest[t][:], ex[t][:, first:S])
+                if t < 2:
+                    nc.scalar.activation(own[t][:, lo:hi], s_ps[:], ACT.Exp, scale=1.0 / 32.0)
+            if t >= 2:
+                nc.sync.dma_start(own[t][:], ex[t][:])
 
         nc.vector.tensor_copy(
             w_wq[:].rearrange("p (t c i) -> p c t i", t=PACK, i=4),
@@ -137,18 +136,15 @@ def tile_picked_localsm_none_po_kernel(tc, x_words, x_scales, d_words, d_scales,
         o_scales = sb("o_scales", [P, S], U8)
         out_rows = out_0.rearrange("(p t) j -> p t j", t=PACK)
 
-        def gathers(c):
-            lo, hi = CHUNKS[c]
-            den[c] = sb(f"den{c}", [P, PACK, hi - lo], F32)
-            part = sb(f"part{c}", [P, PACK, hi - lo], F32)
-            cols = slice(lo // 16, hi // 16)
-            for t in range(PACK):
-                mine = own[0][t][:] if c == 0 else rest[t][:, lo - first : hi - first]
-                nc.vector.tensor_tensor(part[:, t, :], ex[t][:].indirect(n1_t[:, cols]), mine, ALU.add)
-                if t > 0:
-                    nc.vector.tensor_tensor(den[c][:, t - 1, :], ex[t - 1][:].indirect(n2_t[:, cols]), part[:, t - 1, :], ALU.add)
-            t = PACK - 1
-            nc.vector.tensor_tensor(den[c][:, t, :], ex[t][:].indirect(n2_t[:, cols]), part[:, t, :], ALU.add)
+        def gathers(t):
+            den[t] = sb(f"den{t}", [P, S], F32)
+            part = sb(f"part{t}", [P, S], F32, tag="w_ww" if t == 0 else None)
+            for lo, hi in CHUNKS:
+                picks = n1_t[:, lo // 16 : hi // 16]
+                nc.vector.tensor_tensor(part[:, lo:hi], ex[t][:].indirect(picks), own[t][:, lo:hi], ALU.add)
+            for lo, hi in CHUNKS:
+                picks = n2_t[:, lo // 16 : hi // 16]
+                nc.vector.tensor_tensor(den[t][:, lo:hi], ex[t][:].indirect(picks), part[:, lo:hi], ALU.add)
 
         exg_all = sb("exg_all", [P, PACK, S], F32)
 
@@ -156,12 +152,14 @@ def tile_picked_localsm_none_po_kernel(tc, x_words, x_scales, d_words, d_scales,
             for t in range(PACK):
                 nc.scalar.activation(exg_all[:, t, :], ex[t][:], ACT.Copy, scale=gn_t[:, t : t + 1])
 
-        def invert(c):
-            lo, hi = CHUNKS[c]
-            r = sb(f"r{c}", [P, PACK, hi - lo], F32)
+        for c, (lo, hi) in enumerate(CHUNKS):
             r2[c] = sb(f"r2{c}", [P, PACK, hi - lo], F32)
-            nc.scalar.activation(r[:], den[c][:], ACT.Abs_reciprocal_sqrt, scale=0.5)
-            nc.scalar.activation(r2[c][:], r[:], ACT.Square)
+
+        def invert(t):
+            for c, (lo, hi) in enumerate(CHUNKS):
+                r = sb(f"r{t}_{c}", [P, hi - lo], F32, tag=f"r{t}")
+                nc.scalar.activation(r[:], den[t][:, lo:hi], ACT.Abs_reciprocal_sqrt, scale=0.5)
+                nc.scalar.activation(r2[c][:, t, :], r[:], ACT.Square)
 
         units = S // UNIT
         zb = {}
@@ -182,14 +180,15 @@ def tile_picked_localsm_none_po_kernel(tc, x_words, x_scales, d_words, d_scales,
             zs[u] = sb(f"zs{u}", [P, UNIT], U8)
             nc.vector.quantize_mx(out=zq[u][:].bitcast(FP8X4), scales=zs[u][:], in_=zb[u][:])
 
-        o_sb, ob = {}, {}
+        o_ps, o_sb = {}, {}
+        ob = {}
 
         def product(u):
-            o_ps = psum.tile([P, PACK, UNIT], F32, name=f"o{u}", tag=f"bank{(u + 5) % 8}")
+            o_ps[u] = psum.tile([P, PACK, UNIT], F32, name=f"o{u}", tag=f"bank{(u + 5) % 8}")
             for t in range(PACK):
                 cols = slice(P * t, P * (t + 1))
                 nc.tensor.matmul_mx(
-                    o_ps[:, t, :],
+                    o_ps[u][:, t, :],
                     lhsT=w_wq[:, cols].bitcast(FP8X4),
                     lhsT_scale=w_sq[:, cols],
                     rhs=zq[u][:].bitcast(FP8X4),
@@ -197,40 +196,51 @@ def tile_picked_localsm_none_po_kernel(tc, x_words, x_scales, d_words, d_scales,
                     start=True,
                     stop=True,
                 )
-            o_sb[u] = sb(f"o_sb{u}", [P, PACK, UNIT], F32)
-            nc.scalar.copy(o_sb[u][:], o_ps[:])
+
+        def store(u):
+            o_sb[u] = sb(f"o_sb{u}", [P, PACK, UNIT], F32, tag="r3" if u == 0 else None)
+            nc.scalar.copy(o_sb[u][:], o_ps[u][:])
             nc.sync.dma_start(out_rows[:, :, u * UNIT : (u + 1) * UNIT], o_sb[u][:])
 
-        def round_out(u):
-            ob[u] = sb(f"ob{u}", [P, UNIT * PACK], BF16)
+        def round_out(u, source):
+            pair = u // 2
+            if pair not in ob:
+                ob[pair] = sb(f"ob{pair}", [P, 2, UNIT * PACK], BF16, tag="zb3" if pair == 0 else None)
             nc.vector.tensor_copy(
-                ob[u][:].rearrange("p (c i t) -> p c t i", i=2, t=PACK),
-                o_sb[u][:].rearrange("p t (c i) -> p c t i", i=2),
+                ob[pair][:, u % 2, :].rearrange("p (c i t) -> p c t i", i=2, t=PACK),
+                source[:].rearrange("p t (c i) -> p c t i", i=2),
             )
 
-        def pack_out(u):
-            cols = slice(u * UNIT, (u + 1) * UNIT)
-            nc.vector.quantize_mx(out=o_codes[:, cols].bitcast(FP8X4), scales=o_scales[:, cols], in_=ob[u][:])
-            if u % 2 == 1:
-                pair = slice((u - 1) * UNIT, (u + 1) * UNIT)
-                nc.sync.dma_start(words_of(out_1)[:, pair], o_codes[:, pair])
+        def pack_out(pair):
+            cols = slice(2 * pair * UNIT, 2 * (pair + 1) * UNIT)
+            nc.vector.quantize_mx(
+                out=o_codes[:, cols].bitcast(FP8X4),
+                scales=o_scales[:, cols],
+                in_=ob[pair][:].rearrange("p u w -> p (u w)"),
+            )
+            nc.sync.dma_start(words_of(out_1)[:, cols], o_codes[:, cols])
 
         weigh()
-        for c in range(len(CHUNKS)):
-            gathers(c)
-        for c in range(len(CHUNKS)):
-            invert(c)
+        for t in range(PACK):
+            gathers(t)
+        for t in range(PACK):
+            invert(t)
         for u in range(units + 1):
             if u < units:
                 share(u)
             if u > 0:
                 pack(u - 1)
                 product(u - 1)
-        for u in range(units + 1):
-            if u < units:
-                round_out(u)
-            if u > 0:
-                pack_out(u - 1)
+        last = units - 1
+        for u in range(last):
+            store(u)
+        round_out(0, o_sb[0])
+        round_out(1, o_sb[1])
+        round_out(last, o_ps[last])
+        store(last)
+        round_out(2, o_sb[2])
+        pack_out(0)
+        pack_out(1)
         for q in range(4):
             eng = nc.sync if q % 2 == 0 else nc.scalar
             eng.dma_start(out_2[0, 4 * q : 4 * q + 4, :].bitcast(I32), o_scales[32 * q : 32 * q + 4, :].bitcast(I32))

from contextlib import ExitStack

import concourse.mybir as mybir

K, T, S, N, G, H = 512, 2048, 512, 512, 2048, 512
FLOPS = 2 * K * H * S + 2 * H * N * S

F32 = mybir.dt.float32
BF16 = mybir.dt.bfloat16
I32 = mybir.dt.int32
U32 = mybir.dt.uint32
U16 = mybir.dt.uint16
U8 = mybir.dt.uint8
FP8X4 = mybir.dt.float8_e4m3fn_x4
ACT = mybir.ActivationFunctionType
ALU = mybir.AluOpType

P = 128
PACK = 4
UNIT = 128
CHUNKS = ((0, 256), (256, 512))


def tile_picked_localsm_none_po_kernel(tc, x_words, x_scales, d_words, d_scales, gn, w1_words, w1_scales, offs, kidx, n1, n2, out_0, out_1, out_2):
    nc = tc.nc
    with ExitStack() as ctx:
        lists = ctx.enter_context(tc.tile_pool(name="lists", bufs=1))
        held = ctx.enter_context(tc.tile_pool(name="held", bufs=1))
        psum = ctx.enter_context(tc.psum_pool(name="psum", bufs=1))

        def sb(name, shape, dtype, tag=None):
            return held.tile(shape, dtype, name=name, tag=tag or name, align_bytes=64)

        def words_of(ap):
            return ap[0].rearrange("p n t -> p (n t)").bitcast(I32)

        kidx_t = lists.tile([P, H // 16], U16, name="kidx_t")
        offs_t = lists.tile([P, S // 16], U16, name="offs_t")
        n1_t = lists.tile([P, S // 16], U16, name="n1_t")
        n2_t = lists.tile([P, S // 16], U16, name="n2_t")

        d_sw = sb("d_sw", [P, G], U8)
        x_sw = sb("x_sw", [P, T], U8)
        d_ww = sb("d_ww", [P, G], I32)
        x_ww = sb("x_ww", [P, T], I32)
        planes = sb("planes", [P, H], U8)
        w_sw = sb("w_sw", [P, N], U8)
        w_ww = sb("w_ww", [P, N], I32)
        gn_t = sb("gn_t", [P, PACK], F32)

        nc.gpsimd.memset(d_sw[:].bitcast(I32), 0)
        nc.vector.memset(x_sw[:].bitcast(I32), 0)
        nc.vector.memset(planes[:].bitcast(I32), 0)
        nc.vector.memset(w_sw[:].bitcast(I32), 0)

        nc.sync.dma_start(kidx_t[:], kidx)
        nc.sync.dma_start(offs_t[:], offs)
        nc.sync.dma_start(d_sw[0:P:8, :].bitcast(I32), d_scales[0].bitcast(I32))
        for q in range(4):
            nc.sync.dma_start(x_sw[32 * q : 32 * q + 4, :].bitcast(I32), x_scales[0, 4 * q : 4 * q + 4, :].bitcast(I32))
        nc.sync.dma_start(d_ww[:], words_of(d_words))
        nc.sync.dma_start(x_ww[:], words_of(x_words))
        nc.sync.dma_start(n1_t[:], n1)
        nc.sync.dma_start(n2_t[:], n2)

        d_sg = sb("d_sg", [P, H], U8)
        x_sg = sb("x_sg", [P, S], U8)
        staged = sb("staged", [P, H], U8)
        nc.vector.tensor_copy(d_sg[:], d_sw[:].indirect(kidx_t[:]))
        nc.vector.tensor_copy(
            staged[:].rearrange("p (t c i) -> p c t i", t=PACK, i=16),
            d_sg[:].rearrange("p (c i t) -> p c t i", t=PACK, i=16),
        )
        for q in range(4):
            nc.scalar.dma_start(
                planes[32 * q : 32 * q + 4, :].bitcast(I32), staged[32 * q : 32 * q + 32 : 8, :].bitcast(I32)
            )
        nc.vector.tensor_copy(x_sg[:], x_sw[:].indirect(offs_t[:]))

        nc.sync.dma_start(w_ww[:], words_of(w1_words))
        for q in range(4):
            nc.sync.dma_start(w_sw[32 * q : 32 * q + 4, :].bitcast(I32), w1_scales[0, 4 * q : 4 * q + 4, :].bitcast(I32))
        nc.sync.dma_start(gn_t[:], gn.rearrange("(p t) o -> p (t o)", t=PACK))

        d_wg = sb("d_wg", [P, H], I32)
        x_wg = sb("x_wg", [P, S], I32)
        d_wq = sb("d_wq", [P, H], I32)
        nc.vector.tensor_copy(d_wg[:].bitcast(U32), d_ww[:].bitcast(U32).indirect(kidx_t[:]))
        nc.vector.tensor_copy(
            d_wq[:].rearrange("p (t c i) -> p c t i", t=PACK, i=4),
            d_wg[:].rearrange("p (c i t) -> p c t i", t=PACK, i=4),
        )
        half = S // 2
        for lo in (0, half):
            nc.vector.tensor_copy(
                x_wg[:, lo : lo + half].bitcast(U32),
                x_ww[:].bitcast(U32).indirect(offs_t[:, lo // 16 : (lo + half) // 16]),
            )

        w_wq = sb("w_wq", [P, N], I32)
        w_sq = sb("w_sq", [P, N], U8)

        ex = [sb(f"ex{t}", [P, S], F32) for t in range(PACK)]
        own = [sb(f"own{t}", [P, S], F32) for t in range(PACK)]
        for t in range(PACK):
            cols = slice(P * t, P * (t + 1))
            pieces = ((0, half), (half, S)) if t == 0 else ((0, S),)
            for lo, hi in pieces:
                s_ps = psum.tile([P, hi - lo], F32, name=f"s{t}_{lo}", tag=f"bank{t}" if lo == 0 else "bank4")
                nc.tensor.matmul_mx(
                    s_ps[:],
                    lhsT=d_wq[:, cols].bitcast(FP8X4),
                    lhsT_scale=planes[:, cols],
                    rhs=x_wg[:, lo:hi].bitcast(FP8X4),
                    rhs_scale=x_sg[:, lo:hi],
                    start=True,
                    stop=True,
                )
                nc.scalar.activation(ex[t][:, lo:hi], s_ps[:], ACT.Exp, scale=1.0 / 32.0)
                if t < 2:
                    nc.scalar.activation(own[t][:, lo:hi], s_ps[:], ACT.Exp, scale=1.0 / 32.0)
            if t >= 2:
                nc.sync.dma_start(own[t][:], ex[t][:])

        nc.vector.tensor_copy(
            w_wq[:].rearrange("p (t c i) -> p c t i", t=PACK, i=4),
            w_ww[:].rearrange("p (c i t) -> p c t i", t=PACK, i=4),
        )
        nc.vector.tensor_copy(
            w_sq[:].rearrange("p (t c i) -> p c t i", t=PACK, i=16),
            w_sw[:].rearrange("p (c i t) -> p c t i", t=PACK, i=16),
        )

        den, r2, zq, zs = {}, {}, {}, {}
        o_codes = sb("o_codes", [P, S], I32)
        o_scales = sb("o_scales", [P, S], U8)
        out_rows = out_0.rearrange("(p t) j -> p t j", t=PACK)

        def gathers(t):
            den[t] = sb(f"den{t}", [P, S], F32)
            part = sb(f"part{t}", [P, S], F32, tag="w_ww" if t == 0 else None)
            for lo, hi in CHUNKS:
                picks = n1_t[:, lo // 16 : hi // 16]
                nc.vector.tensor_tensor(part[:, lo:hi], ex[t][:].indirect(picks), own[t][:, lo:hi], ALU.add)
            for lo, hi in CHUNKS:
                picks = n2_t[:, lo // 16 : hi // 16]
                nc.vector.tensor_tensor(den[t][:, lo:hi], ex[t][:].indirect(picks), part[:, lo:hi], ALU.add)

        exg_all = sb("exg_all", [P, PACK, S], F32)

        def weigh():
            for t in range(PACK):
                nc.scalar.activation(exg_all[:, t, :], ex[t][:], ACT.Copy, scale=gn_t[:, t : t + 1])

        for c, (lo, hi) in enumerate(CHUNKS):
            r2[c] = sb(f"r2{c}", [P, PACK, hi - lo], F32)

        def invert(t):
            for c, (lo, hi) in enumerate(CHUNKS):
                r = sb(f"r{t}_{c}", [P, hi - lo], F32, tag=f"r{t}")
                nc.scalar.activation(r[:], den[t][:, lo:hi], ACT.Abs_reciprocal_sqrt, scale=0.5)
                nc.scalar.activation(r2[c][:, t, :], r[:], ACT.Square)

        units = S // UNIT
        zb = {}

        def share(u):
            c = [lo <= u * UNIT < hi for lo, hi in CHUNKS].index(True)
            j0 = u * UNIT - CHUNKS[c][0]
            zb[u] = sb(f"zb{u}", [P, UNIT * PACK], BF16)
            nc.vector.tensor_tensor(
                zb[u][:].rearrange("p (c i t) -> p c t i", i=2, t=PACK),
                r2[c][:, :, j0 : j0 + UNIT].rearrange("p t (c i) -> p c t i", i=2),
                exg_all[:, :, u * UNIT : (u + 1) * UNIT].rearrange("p t (c i) -> p c t i", i=2),
                ALU.mult,
            )

        def pack(u):
            zq[u] = sb(f"zq{u}", [P, UNIT], I32)
            zs[u] = sb(f"zs{u}", [P, UNIT], U8)
            nc.vector.quantize_mx(out=zq[u][:].bitcast(FP8X4), scales=zs[u][:], in_=zb[u][:])

        o_ps, o_sb = {}, {}
        ob = {}

        def product(u):
            o_ps[u] = psum.tile([P, PACK, UNIT], F32, name=f"o{u}", tag=f"bank{(u + 5) % 8}")
            for t in range(PACK):
                cols = slice(P * t, P * (t + 1))
                nc.tensor.matmul_mx(
                    o_ps[u][:, t, :],
                    lhsT=w_wq[:, cols].bitcast(FP8X4),
                    lhsT_scale=w_sq[:, cols],
                    rhs=zq[u][:].bitcast(FP8X4),
                    rhs_scale=zs[u][:],
                    start=True,
                    stop=True,
                )

        def store(u):
            o_sb[u] = sb(f"o_sb{u}", [P, PACK, UNIT], F32, tag="r3" if u == 0 else None)
            nc.scalar.copy(o_sb[u][:], o_ps[u][:])
            nc.sync.dma_start(out_rows[:, :, u * UNIT : (u + 1) * UNIT], o_sb[u][:])

        def round_out(u, source):
            pair = u // 2
            if pair not in ob:
                ob[pair] = sb(f"ob{pair}", [P, 2, UNIT * PACK], BF16, tag="zb3" if pair == 0 else None)
            nc.vector.tensor_copy(
                ob[pair][:, u % 2, :].rearrange("p (c i t) -> p c t i", i=2, t=PACK),
                source[:].rearrange("p t (c i) -> p c t i", i=2),
            )

        def pack_out(pair):
            cols = slice(2 * pair * UNIT, 2 * (pair + 1) * UNIT)
            nc.vector.quantize_mx(
                out=o_codes[:, cols].bitcast(FP8X4),
                scales=o_scales[:, cols],
                in_=ob[pair][:].rearrange("p u w -> p (u w)"),
            )
            nc.sync.dma_start(words_of(out_1)[:, cols], o_codes[:, cols])

        weigh()
        for t in range(PACK):
            gathers(t)
        for t in range(PACK):
            invert(t)
        for u in range(units + 1):
            if u < units:
                share(u)
            if u > 0:
                pack(u - 1)
                product(u - 1)
        last = units - 1
        for u in range(last):
            store(u)
        round_out(0, o_sb[0])
        round_out(1, o_sb[1])
        round_out(last, o_ps[last])
        store(last)
        round_out(2, o_sb[2])
        pack_out(0)
        pack_out(1)
        for q in range(4):
            eng = nc.sync if q % 2 == 0 else nc.scalar
            eng.dma_start(out_2[0, 4 * q : 4 * q + 4, :].bitcast(I32), o_scales[32 * q : 32 * q + 4, :].bitcast(I32))
